import numpy as np
import ml_dtypes


def mxq(x, axis, fmt="e4m3"):
    dtype, down = {"e4m3": (ml_dtypes.float8_e4m3fn, 7), "e5m2": (ml_dtypes.float8_e5m2, 14)}[fmt]
    v = np.moveaxis(np.asarray(x, np.float32).astype(ml_dtypes.bfloat16).astype(np.float64), axis, -1)
    blocks = v.reshape(v.shape[:-1] + (-1, 32))
    amax = np.abs(blocks).max(-1, keepdims=True)
    byte = np.maximum(np.where(amax > 0, np.frexp(amax)[1] - 1 + 127, 0) - down, 1)
    scale = np.exp2(byte - 127.0)
    codes = (blocks / scale).astype(np.float32).astype(dtype).astype(np.float64)
    return np.moveaxis((codes * scale).reshape(v.shape), -1, axis)


WIDE = False


def mx_kscale(k):
    if not WIDE:
        return np.ones(k)
    levels = np.array([30, -30])
    if k % 512:
        return np.exp2(np.random.permutation(np.resize(levels, k // 32))).repeat(32)
    a = np.empty((k // 512, 16))
    for p in range(k // 512):
        a[p, :8] = np.random.permutation(np.resize(levels, 8))
        for g in range(8):
            far = levels[np.abs(levels - a[p, g]) >= 10]
            a[p, g + 8] = far[np.random.randint(len(far))]
    return np.exp2(a.ravel()).repeat(32)


def f64(x):
    return np.asarray(x).astype(np.float64)


def striped(idx):
    return np.tile(np.asarray(idx).reshape(-1, 16).T, (8, 1)).astype(np.uint16)


def unstriped(offs):
    return offs[:16].T.reshape(-1).astype(np.int64)


E2M1 = np.array([0.0, 0.5, 1.0, 1.5, 2.0, 3.0, 4.0, 6.0, -0.0, -0.5, -1.0, -1.5, -2.0, -3.0, -4.0, -6.0])


def pack_weight(w, fmt):
    k, n = w.shape
    w = f64(np.asarray(w, np.float32).astype(ml_dtypes.bfloat16)).reshape(k // 32, 32, n)
    amax = np.abs(w).max(1)
    if fmt in ("e4m3", "e5m2"):
        byte = np.frexp(amax)[1] - 1 + 127 - (7 if fmt == "e4m3" else 14)
    else:
        mant, ex = np.frexp(amax / 6.0)
        byte = np.where(mant > 0.5, ex, ex - 1) + 127
    byte = np.clip(np.where(amax > 0, byte, 1), 1, 254)
    scaled = (w * np.exp2(127.0 - byte)[:, None, :]).reshape(k, n).astype(np.float32)
    by_word = np.ascontiguousarray(scaled.reshape(k // 512, 128, 4, n).transpose(0, 1, 3, 2))
    if fmt in ("e4m3", "e5m2"):
        words = by_word.astype(ml_dtypes.float8_e4m3fn if fmt == "e4m3" else ml_dtypes.float8_e5m2).view(np.uint8)
    else:
        c = by_word.astype(ml_dtypes.float4_e2m1fn).view(np.uint8) & 0xF
        words = (c[..., 0::2] | (c[..., 1::2] << 4)).reshape(k // 512, 128, 2 * n)
    return np.ascontiguousarray(words), np.ascontiguousarray(byte.astype(np.uint8).reshape(k // 512, 16, n))


def unpack_weight(words, scales, fmt):
    g, _, n = scales.shape
    words = np.ascontiguousarray(words).reshape(g, 128, n, -1)
    if fmt in ("e4m3", "e5m2"):
        vals = words.view(ml_dtypes.float8_e4m3fn if fmt == "e4m3" else ml_dtypes.float8_e5m2).astype(np.float64)
    else:
        nib = np.empty((g, 128, n, 4), np.uint8)
        nib[..., 0::2] = words & 0xF
        nib[..., 1::2] = words >> 4
        vals = E2M1[nib]
    vals = vals * np.repeat(np.exp2(scales.astype(np.float64) - 127.0), 8, axis=1)[..., None]
    return vals.transpose(0, 1, 3, 2).reshape(g * 512, n)


def bf(x):
    return np.asarray(x, np.float32).astype(ml_dtypes.bfloat16)


def planes(Y):
    r, m = Y.shape
    b = f64(bf(Y)).reshape(r // 32, 32, m)
    amax = np.abs(b).max(1)
    byte = np.clip(np.where(amax > 0, np.frexp(amax)[1] - 1 + 127 - 7, 1), 1, 254)
    codes = (b * np.exp2(127.0 - byte)[:, None, :]).reshape(r, m).astype(np.float32).astype(ml_dtypes.float8_e4m3fn).view(np.uint8)
    words = codes.reshape(r // 512, 128, 4, m).transpose(0, 1, 3, 2)
    return np.ascontiguousarray(words), np.ascontiguousarray(byte.astype(np.uint8).reshape(r // 512, 16, m))


K, T, J, R, F, Z, V, N, C = 512, 512, 256, 512, 512, 1024, 512, 512, 512


def setup_inputs():
    n = np.random.standard_normal
    idx = np.random.permutation(T)[:J]
    idx2 = np.random.permutation(Z)[:J]
    idx3 = np.random.permutation(V)[:J]
    idx4 = np.random.permutation(C)[:J]
    fk = mx_kscale(K)
    fr = mx_kscale(R)
    ff = mx_kscale(F)
    wp = pack_weight(n((K, R)) * 1 / np.sqrt(K) * fk[:, None] * fr, "e5m2")
    w2p = pack_weight(n((F, R)) * 1 / np.sqrt(F) * ff[:, None] * fr, "e5m2")
    wbp = pack_weight(n((R, N)) * 1 / np.sqrt(R) / fr[:, None], "e4m3")
    return {
        "xf": (n((K, T))).astype(np.float32),
        "ow": (n((K, J)) * 0.7).astype(np.float32),
        "fk": (np.random.uniform(0.5, 2.0, (K, 1)) / fk[:, None]).astype(np.float32),
        "w_words": wp[0],
        "w_scales": wp[1],
        "xo": (n((F, Z))).astype(np.float32),
        "fl": (np.random.uniform(0.5, 2.0, (F, 1)) / ff[:, None]).astype(np.float32),
        "so": (n((F, J)) * 0.8).astype(np.float32),
        "w2_words": w2p[0],
        "w2_scales": w2p[1],
        "tb": (n((R, V)) * 0.7 * fr[:, None]).astype(np.float32),
        "wb_words": wbp[0],
        "wb_scales": wbp[1],
        "tz": (n((N, C)) * 0.6).astype(np.float32),
        "rw": (np.random.uniform(0.5, 2.0, (1, J))).astype(np.float32),
        "offs": striped(idx),
        "offs2": striped(idx2),
        "offs3": striped(idx3),
        "offs4": striped(idx4),
    }


def reference(xf, ow, fk, w_words, w_scales, xo, fl, so, w2_words, w2_scales, tb, wb_words, wb_scales, tz, rw, offs, offs2, offs3, offs4):
    idx = unstriped(offs)
    idx2 = unstriped(offs2)
    idx3 = unstriped(offs3)
    idx4 = unstriped(offs4)
    wu = unpack_weight(w_words, w_scales, "e5m2")
    w2u = unpack_weight(w2_words, w2_scales, "e5m2")
    wbu = unpack_weight(wb_words, wb_scales, "e4m3")
    u = (f64(xf)[:, idx] - f64(ow)) * f64(fk)
    u2 = np.maximum(f64(xo)[:, idx2], f64(so)) * f64(fl)
    uq = mxq(u, 0, "e5m2")
    u2q = mxq(u2, 0, "e4m3")
    a = wu.T @ uq + w2u.T @ u2q
    hid = np.maximum(a - f64(tb)[:, idx3], 0.0)
    hidq = mxq(hid, 0, "e5m2")
    p = wbu.T @ hidq
    y = np.maximum(p, f64(tz)[:, idx4]) * f64(rw)
    words, scales = planes(y)
    return y, words, scales

@@ -1,0 +1,217 @@
+from contextlib import ExitStack
+
+import concourse.mybir as mybir
+from concourse.masks import make_identity
+
+F32 = mybir.dt.float32
+BF16 = mybir.dt.bfloat16
+I32 = mybir.dt.int32
+U32 = mybir.dt.uint32
+U16 = mybir.dt.uint16
+U8 = mybir.dt.uint8
+E4M3 = mybir.dt.float8_e4m3fn_x4
+E5M2 = mybir.dt.float8_e5m2_x4
+ALU = mybir.AluOpType
+ACT = mybir.ActivationFunctionType
+
+P = 128
+PACK = 4
+J = 256
+HALVES = 2
+JH = J // HALVES
+RUN = 4
+COLS = 512
+
+FLOPS = 3 * 2 * 512 * 512 * J
+
+
+def tile_list_sum_offsetpicks_largest_overtable_floored_pl_kernel(
+    tc, xf, ow, fk, w_words, w_scales, xo, fl, so, w2_words, w2_scales, tb, wb_words, wb_scales, tz, rw,
+    offs, offs2, offs3, offs4, out_0, out_1, out_2,
+):
+    nc = tc.nc
+
+    def dealt(dram):
+        return dram.rearrange("(p t) c -> p t c", t=PACK)
+
+    def by_runs(planes):
+        return planes.rearrange("p t (c i) -> p c t i", i=RUN)
+
+    def woven(tile):
+        return tile[:].rearrange("p (c i t) -> p c t i", i=RUN, t=PACK)
+
+    with ExitStack() as ctx:
+        keep = ctx.enter_context(tc.tile_pool(name="keep", bufs=1))
+        psum = ctx.enter_context(tc.psum_pool(name="psum", bufs=1))
+
+        def load_list(dram, name):
+            tile = keep.tile([P, J // 16], U16, name=name)
+            nc.sync.dma_start(tile[:], dram)
+            return tile
+
+        def load_plane(dram, t, name):
+            tile = keep.tile([P, dram.shape[1]], F32, name="%s%d" % (name, t))
+            nc.sync.dma_start(tile[:], dealt(dram)[:, t, :])
+            return tile
+
+        def load_planes(dram, name):
+            tile = keep.tile([P, PACK, dram.shape[1]], F32, name=name)
+            nc.sync.dma_start(tile[:], dealt(dram))
+            return tile
+
+        def load_words(dram, name):
+            tile = keep.tile([P, COLS], I32, name=name)
+            nc.sync.dma_start(tile[:], dram[0].rearrange("p n t -> p (n t)").bitcast(I32))
+            return tile
+
+        def load_factor(dram, name):
+            tile = keep.tile([P, PACK], F32, name=name)
+            nc.gpsimd.dma_start(tile[:], dram.rearrange("(p t) o -> p (t o)", t=PACK))
+            return tile
+
+        def deal_words(raw, name):
+            tile = keep.tile([P, PACK, P], U32, name=name, align_bytes=64)
+            nc.scalar.copy(by_runs(tile[:]), raw[:].bitcast(U32).rearrange("p (c i t) -> p c t i", i=RUN, t=PACK))
+            return tile
+
+        def quantise(src, width, fmt, name):
+            codes = keep.tile([P, width], U32, name=name + "_codes", align_bytes=64)
+            scales = keep.tile([P, width], U8, name=name + "_scales", align_bytes=64)
+            nc.vector.quantize_mx(out=codes[:].bitcast(fmt), scales=scales[:], in_=src[:])
+            return codes, scales
+
+        def halves():
+            return [(h, slice(h * JH, (h + 1) * JH)) for h in range(HALVES)]
+
+        scale_rows = keep.tile([P, 3, COLS], U8, name="scale_rows")
+        nc.vector.memset(scale_rows[:].bitcast(U32), 0)
+        for n, dram in enumerate((w_scales, w2_scales, wb_scales)):
+            nc.scalar.dma_start(scale_rows[0:16, n, :].bitcast(I32), dram[0].bitcast(I32))
+        fk_sb = load_factor(fk, "fk_sb")
+        fl_sb = load_factor(fl, "fl_sb")
+
+        list1 = load_list(offs, "list1")
+        ow_sb = load_planes(ow, "ow_sb")
+        xf_sb = [load_plane(xf, t, "xf") for t in range(PACK)]
+        list2 = load_list(offs2, "list2")
+        so_sb = load_planes(so, "so_sb")
+        xo_sb = [load_plane(xo, t, "xo") for t in range(PACK)]
+        w_raw = load_words(w_words, "w_raw")
+        w2_raw = load_words(w2_words, "w2_raw")
+        list3 = load_list(offs3, "list3")
+        tb_sb = [load_plane(tb, t, "tb") for t in range(PACK)]
+        wb_raw = load_words(wb_words, "wb_raw")
+        list4 = load_list(offs4, "list4")
+        tz_sb = [load_plane(tz, t, "tz") for t in range(PACK)]
+
+        w_sc = keep.tile([P, 3, COLS], U8, name="w_sc", align_bytes=64)
+        nc.vector.tensor_copy(
+            w_sc[:].rearrange("p n (t m) -> p n t m", t=PACK),
+            scale_rows[:].rearrange("p n (m t) -> p n t m", t=PACK),
+        )
+        w_sc_words = w_sc[:].rearrange("p n c -> p (n c)").bitcast(I32)
+        for q in range(1, 4):
+            nc.scalar.dma_start(w_sc_words[32 * q : 32 * q + 4, :], w_sc_words[4 * q : 4 * q + 4, :])
+
+        rw_col = keep.tile([P, 2], F32, name="rw_col")
+        nc.gpsimd.dma_start(rw_col[:], rw[0].rearrange("(p e) -> p e", e=2))
+        ident = keep.tile([P, P], F32, name="ident")
+        make_identity(nc, ident[:])
+        rw_ps = psum.tile([P, 2, P], F32, name="rw_ps")
+        for e in range(2):
+            nc.tensor.transpose(rw_ps[:, e, :], rw_col[:, e : e + 1].to_broadcast([P, P]), ident[:])
+
+        def factor(tile, width):
+            return tile[:].unsqueeze(1).unsqueeze(3).to_broadcast([P, width // RUN, PACK, RUN])
+
+        diff = keep.tile([P, PACK, J], F32, name="diff")
+        for t in range(PACK):
+            nc.vector.tensor_tensor(diff[:, t, :], xf_sb[t][:].indirect(list1[:]), ow_sb[:, t, :], ALU.subtract)
+        u_bf = keep.tile([P, J * PACK], BF16, name="u_bf", align_bytes=64)
+        nc.vector.tensor_tensor(woven(u_bf), by_runs(diff[:]), factor(fk_sb, J), ALU.mult)
+        u_codes, u_scales = quantise(u_bf, J, E5M2, "u")
+
+        xo_pick = keep.tile([P, PACK, J], F32, name="xo_pick")
+        larger = keep.tile([P, PACK, J], F32, name="larger")
+        for t in range(PACK):
+            nc.scalar.activation(xo_pick[:, t, :], xo_sb[t][:].indirect(list2[:]), ACT.Copy)
+            nc.vector.tensor_tensor(larger[:, t, :], xo_pick[:, t, :], so_sb[:, t, :], ALU.max)
+        u2_bf = []
+        for h, js in halves():
+            tile = keep.tile([P, JH * PACK], BF16, name="u2_bf%d" % h, align_bytes=64)
+            nc.vector.tensor_tensor(woven(tile), by_runs(larger[:, :, js]), factor(fl_sb, JH), ALU.mult)
+            u2_bf.append(tile)
+        u2_q = [quantise(u2_bf[h], JH, E4M3, "u2_%d" % h) for h, js in halves()]
+
+        w_sb = deal_words(w_raw, "w_sb")
+        w2_sb = deal_words(w2_raw, "w2_sb")
+
+        def weight_scales(n, t):
+            return w_sc[:, n, t * P : (t + 1) * P]
+
+        a_ps = []
+        for h, js in halves():
+            bank = psum.tile([P, PACK, JH], F32, name="a_ps%d" % h)
+            for t in range(PACK):
+                nc.tensor.matmul_mx(
+                    bank[:, t, :], lhsT=w_sb[:, t, :].bitcast(E5M2), lhsT_scale=weight_scales(0, t),
+                    rhs=u_codes[:, js].bitcast(E5M2), rhs_scale=u_scales[:, js], start=(t == 0), stop=False,
+                )
+            a_ps.append(bank)
+        for h, js in halves():
+            codes, scales = u2_q[h]
+            for t in range(PACK):
+                nc.tensor.matmul_mx(
+                    a_ps[h][:, t, :], lhsT=w2_sb[:, t, :].bitcast(E5M2), lhsT_scale=weight_scales(1, t),
+                    rhs=codes[:].bitcast(E4M3), rhs_scale=scales[:], start=False, stop=(t == PACK - 1),
+                )
+
+        tb_pick = keep.tile([P, PACK, J], F32, name="tb_pick")
+        for t in range(PACK):
+            nc.scalar.activation(tb_pick[:, t, :], tb_sb[t][:].indirect(list3[:]), ACT.Copy)
+        hid_bf = []
+        for h, js in halves():
+            over = keep.tile([P, PACK, JH], F32, name="over%d" % h)
+            nc.vector.tensor_tensor(over[:], a_ps[h][:], tb_pick[:, :, js], ALU.subtract)
+            tile = keep.tile([P, JH * PACK], BF16, name="hid_bf%d" % h, align_bytes=64)
+            nc.scalar.activation(woven(tile), by_runs(over[:]), ACT.Relu)
+            hid_bf.append(tile)
+        wb_sb = deal_words(wb_raw, "wb_sb")
+        p_ps = []
+        for h, js in halves():
+            codes, scales = quantise(hid_bf[h], JH, E5M2, "hid%d" % h)
+            bank = psum.tile([P, PACK, JH], F32, name="p_ps%d" % h)
+            for t in range(PACK):
+                nc.tensor.matmul_mx(
+                    bank[:, t, :], lhsT=wb_sb[:, t, :].bitcast(E4M3), lhsT_scale=weight_scales(2, t),
+                    rhs=codes[:].bitcast(E5M2), rhs_scale=scales[:], start=True, stop=True,
+                )
+            p_ps.append(bank)
+
+        tz_pick = keep.tile([P, PACK, J], F32, name="tz_pick")
+        for t in range(PACK):
+            nc.scalar.activation(tz_pick[:, t, :], tz_sb[t][:].indirect(list4[:]), ACT.Copy)
+        y_codes = keep.tile([P, J], U32, name="y_codes", align_bytes=64)
+        y_scales = keep.tile([P, J], U8, name="y_scales", align_bytes=64)
+        out_words = out_1[0].rearrange("p n t -> p (n t)").bitcast(I32)
+        y_bf = []
+        for h, js in halves():
+            floored = keep.tile([P, PACK, JH], F32, name="floored%d" % h)
+            nc.vector.tensor_tensor(floored[:], p_ps[h][:], tz_pick[:, :, js], ALU.max)
+            y = keep.tile([P, PACK, JH], F32, name="y%d" % h)
+            pairs = slice(h * JH // 2, (h + 1) * JH // 2)
+            rw_half = rw_ps[:, :, pairs].rearrange("p e m -> p m e").unsqueeze(1).to_broadcast([P, PACK, JH // 2, 2])
+            nc.vector.tensor_tensor(
+                y[:].rearrange("p t (m e) -> p t m e", e=2), floored[:].rearrange("p t (m e) -> p t m e", e=2),
+                rw_half, ALU.mult,
+            )
+            nc.sync.dma_start(dealt(out_0)[:, :, js], y[:])
+            tile = keep.tile([P, JH * PACK], BF16, name="y_bf%d" % h, align_bytes=64)
+            nc.scalar.copy(woven(tile), by_runs(y[:]))
+            y_bf.append(tile)
+        for h, js in halves():
+            nc.vector.quantize_mx(out=y_codes[:, js].bitcast(E4M3), scales=y_scales[:, js], in_=y_bf[h][:])
+            nc.sync.dma_start(out_words[:, js], y_codes[:, js].bitcast(I32))
+        for q in range(4):
+            queue = nc.sync if q < 2 else nc.scalar
+            queue.dma_start(out_2[0, 4 * q : 4 * q + 4, :].bitcast(I32), y_scales[32 * q : 32 * q + 4, :].bitcast(I32))

@@ -49,15 +49,13 @@ def tile_list_sum_offsetpicks_largest_overtable_floored_pl_kernel(
             nc.sync.dma_start(tile[:], dram)
             return tile
 
-        def load_plane(dram, t, name):
-            tile = keep.tile([P, dram.shape[1]], F32, name="%s%d" % (name, t))
-            nc.sync.dma_start(tile[:], dealt(dram)[:, t, :])
+        def load_planes(dram, first, count, name):
+            tile = keep.tile([P, count, dram.shape[1]], F32, name="%s%d" % (name, first))
+            nc.sync.dma_start(tile[:], dealt(dram)[:, first : first + count, :])
             return tile
 
-        def load_planes(dram, name):
-            tile = keep.tile([P, PACK, dram.shape[1]], F32, name=name)
-            nc.sync.dma_start(tile[:], dealt(dram))
-            return tile
+        def planes_of(tile):
+            return [tile[:, t, :] for t in range(tile.shape[1])]
 
         def load_words(dram, name):
             tile = keep.tile([P, COLS], I32, name=name)
@@ -84,26 +82,20 @@ def tile_list_sum_offsetpicks_largest_overtable_floored_pl_kernel(
             return [(h, slice(h * JH, (h + 1) * JH)) for h in range(HALVES)]
 
         scale_rows = keep.tile([P, 3, COLS], U8, name="scale_rows")
-        nc.vector.memset(scale_rows[:].bitcast(U32), 0)
-        for n, dram in enumerate((w_scales, w2_scales, wb_scales)):
-            nc.scalar.dma_start(scale_rows[0:16, n, :].bitcast(I32), dram[0].bitcast(I32))
+        nc.gpsimd.memset(scale_rows[:].bitcast(U32), 0)
         fk_sb = load_factor(fk, "fk_sb")
         fl_sb = load_factor(fl, "fl_sb")
-
+        xf_sb = planes_of(load_planes(xf, 0, 2, "xf"))
         list1 = load_list(offs, "list1")
-        ow_sb = load_planes(ow, "ow_sb")
-        xf_sb = [load_plane(xf, t, "xf") for t in range(PACK)]
+        for n, dram in enumerate((w_scales, w2_scales, wb_scales)):
+            nc.sync.dma_start(scale_rows[0:16, n, :].bitcast(I32), dram[0].bitcast(I32))
+        xf_sb = xf_sb + planes_of(load_planes(xf, 2, 2, "xf"))
+        xo_sb = planes_of(load_planes(xo, 0, 1, "xo"))
+        ow_sb = load_planes(ow, 0, PACK, "ow")
         list2 = load_list(offs2, "list2")
-        so_sb = load_planes(so, "so_sb")
-        xo_sb = [load_plane(xo, t, "xo") for t in range(PACK)]
-        w_raw = load_words(w_words, "w_raw")
-        w2_raw = load_words(w2_words, "w2_raw")
-        list3 = load_list(offs3, "list3")
-        tb_sb = [load_plane(tb, t, "tb") for t in range(PACK)]
-        wb_raw = load_words(wb_words, "wb_raw")
-        list4 = load_list(offs4, "list4")
-        tz_sb = [load_plane(tz, t, "tz") for t in range(PACK)]
-
+        xo_sb = xo_sb + planes_of(load_planes(xo, 1, 1, "xo"))
+        so_sb = load_planes(so, 0, PACK, "so")
+        xo_sb = xo_sb + planes_of(load_planes(xo, 2, 1, "xo")) + planes_of(load_planes(xo, 3, 1, "xo"))
         w_sc = keep.tile([P, 3, COLS], U8, name="w_sc", align_bytes=64)
         nc.vector.tensor_copy(
             w_sc[:].rearrange("p n (t m) -> p n t m", t=PACK),
@@ -111,7 +103,27 @@ def tile_list_sum_offsetpicks_largest_overtable_floored_pl_kernel(
         )
         w_sc_words = w_sc[:].rearrange("p n c -> p (n c)").bitcast(I32)
         for q in range(1, 4):
-            nc.scalar.dma_start(w_sc_words[32 * q : 32 * q + 4, :], w_sc_words[4 * q : 4 * q + 4, :])
+            nc.sync.dma_start(w_sc_words[32 * q : 32 * q + 4, :], w_sc_words[4 * q : 4 * q + 4, :])
+
+        w_raw = load_words(w_words, "w_raw")
+        w2_raw = load_words(w2_words, "w2_raw")
+        list3 = load_list(offs3, "list3")
+        tb_sb = [planes_of(load_planes(tb, t, 1, "tb"))[0] for t in range(PACK)]
+        wb_raw = load_words(wb_words, "wb_raw")
+        list4 = load_list(offs4, "list4")
+        tz_sb = [planes_of(load_planes(tz, t, 1, "tz"))[0] for t in range(PACK)]
+
+        def pick(windows, offsets, name, split_last, on_vector=()):
+            picked = keep.tile([P, PACK, J], F32, name=name)
+            for t in range(PACK):
+                if split_last and t == PACK - 1:
+                    for h, js in halves():
+                        nc.scalar.activation(picked[:, t, js], windows[t].indirect(offsets[:, h * JH // 16 : (h + 1) * JH // 16]), ACT.Copy)
+                elif t in on_vector:
+                    nc.vector.tensor_copy(picked[:, t, :], windows[t].indirect(offsets[:]))
+                else:
+                    nc.scalar.activation(picked[:, t, :], windows[t].indirect(offsets[:]), ACT.Copy)
+            return picked
 
         rw_col = keep.tile([P, 2], F32, name="rw_col")
         nc.gpsimd.dma_start(rw_col[:], rw[0].rearrange("(p e) -> p e", e=2))
@@ -124,17 +136,16 @@ def tile_list_sum_offsetpicks_largest_overtable_floored_pl_kernel(
         def factor(tile, width):
             return tile[:].unsqueeze(1).unsqueeze(3).to_broadcast([P, width // RUN, PACK, RUN])
 
+        xf_pick = pick(xf_sb, list1, "xf_pick", False)
         diff = keep.tile([P, PACK, J], F32, name="diff")
-        for t in range(PACK):
-            nc.vector.tensor_tensor(diff[:, t, :], xf_sb[t][:].indirect(list1[:]), ow_sb[:, t, :], ALU.subtract)
+        nc.vector.tensor_tensor(diff[:], xf_pick[:], ow_sb[:], ALU.subtract)
         u_bf = keep.tile([P, J * PACK], BF16, name="u_bf", align_bytes=64)
         nc.vector.tensor_tensor(woven(u_bf), by_runs(diff[:]), factor(fk_sb, J), ALU.mult)
         u_codes, u_scales = quantise(u_bf, J, E5M2, "u")
 
-        xo_pick = keep.tile([P, PACK, J], F32, name="xo_pick")
+        xo_pick = pick(xo_sb, list2, "xo_pick", False)
         larger = keep.tile([P, PACK, J], F32, name="larger")
         for t in range(PACK):
-            nc.scalar.activation(xo_pick[:, t, :], xo_sb[t][:].indirect(list2[:]), ACT.Copy)
             nc.vector.tensor_tensor(larger[:, t, :], xo_pick[:, t, :], so_sb[:, t, :], ALU.max)
         u2_bf = []
         for h, js in halves():
@@ -166,52 +177,77 @@ def tile_list_sum_offsetpicks_largest_overtable_floored_pl_kernel(
                     rhs=codes[:].bitcast(E4M3), rhs_scale=scales[:], start=False, stop=(t == PACK - 1),
                 )
 
-        tb_pick = keep.tile([P, PACK, J], F32, name="tb_pick")
-        for t in range(PACK):
-            nc.scalar.activation(tb_pick[:, t, :], tb_sb[t][:].indirect(list3[:]), ACT.Copy)
-        hid_bf = []
-        for h, js in halves():
-            over = keep.tile([P, PACK, JH], F32, name="over%d" % h)
-            nc.vector.tensor_tensor(over[:], a_ps[h][:], tb_pick[:, :, js], ALU.subtract)
-            tile = keep.tile([P, JH * PACK], BF16, name="hid_bf%d" % h, align_bytes=64)
-            nc.scalar.activation(woven(tile), by_runs(over[:]), ACT.Relu)
-            hid_bf.append(tile)
+        groups = (slice(0, PACK - 1), slice(PACK - 1, PACK))
+        tb_pick = pick(tb_sb, list3, "tb_pick", True, on_vector=(2,))
         wb_sb = deal_words(wb_raw, "wb_sb")
-        p_ps = []
-        for h, js in halves():
+        over = [keep.tile([P, PACK, JH], F32, name="over%d" % h) for h, js in halves()]
+        hid_bf = [keep.tile([P, JH * PACK], BF16, name="hid_bf%d" % h, align_bytes=64) for h, js in halves()]
+        p_ps = [psum.tile([P, PACK, JH], F32, name="p_ps%d" % h) for h, js in halves()]
+        cols = [js for h, js in halves()]
+
+        def take_off(h, ts):
+            nc.vector.tensor_tensor(over[h][:, ts, :], a_ps[h][:, ts, :], tb_pick[:, ts, cols[h]], ALU.subtract)
+
+        def keep_positive(h):
+            nc.vector.tensor_scalar_max(woven(hid_bf[h]), by_runs(over[h][:]), 0.0)
+
+        def second_layer(h):
             codes, scales = quantise(hid_bf[h], JH, E5M2, "hid%d" % h)
-            bank = psum.tile([P, PACK, JH], F32, name="p_ps%d" % h)
             for t in range(PACK):
                 nc.tensor.matmul_mx(
-                    bank[:, t, :], lhsT=wb_sb[:, t, :].bitcast(E4M3), lhsT_scale=weight_scales(2, t),
+                    p_ps[h][:, t, :], lhsT=wb_sb[:, t, :].bitcast(E4M3), lhsT_scale=weight_scales(2, t),
                     rhs=codes[:].bitcast(E5M2), rhs_scale=scales[:], start=True, stop=True,
                 )
-            p_ps.append(bank)
 
-        tz_pick = keep.tile([P, PACK, J], F32, name="tz_pick")
-        for t in range(PACK):
-            nc.scalar.activation(tz_pick[:, t, :], tz_sb[t][:].indirect(list4[:]), ACT.Copy)
+        early, late = groups
+        take_off(0, early)
+        take_off(0, late)
+        take_off(1, early)
+        keep_positive(0)
+        take_off(1, late)
+        second_layer(0)
+        keep_positive(1)
+        second_layer(1)
+
+        tz_pick = pick(tz_sb, list4, "tz_pick", True)
+        floored = [keep.tile([P, PACK, JH], F32, name="floored%d" % h) for h, js in halves()]
+        y = [keep.tile([P, PACK, JH], F32, name="y%d" % h) for h, js in halves()]
+        y_bf = [keep.tile([P, JH * PACK], BF16, name="y_bf%d" % h, align_bytes=64) for h, js in halves()]
         y_codes = keep.tile([P, J], U32, name="y_codes", align_bytes=64)
         y_scales = keep.tile([P, J], U8, name="y_scales", align_bytes=64)
         out_words = out_1[0].rearrange("p n t -> p (n t)").bitcast(I32)
-        y_bf = []
-        for h, js in halves():
-            floored = keep.tile([P, PACK, JH], F32, name="floored%d" % h)
-            nc.vector.tensor_tensor(floored[:], p_ps[h][:], tz_pick[:, :, js], ALU.max)
-            y = keep.tile([P, PACK, JH], F32, name="y%d" % h)
+
+        def floor_at(h, ts):
+            nc.vector.tensor_tensor(floored[h][:, ts, :], p_ps[h][:, ts, :], tz_pick[:, ts, cols[h]], ALU.max)
+
+        def weigh(h, ts):
             pairs = slice(h * JH // 2, (h + 1) * JH // 2)
-            rw_half = rw_ps[:, :, pairs].rearrange("p e m -> p m e").unsqueeze(1).to_broadcast([P, PACK, JH // 2, 2])
+            rw_half = rw_ps[:, :, pairs].rearrange("p e m -> p m e").unsqueeze(1)
             nc.vector.tensor_tensor(
-                y[:].rearrange("p t (m e) -> p t m e", e=2), floored[:].rearrange("p t (m e) -> p t m e", e=2),
-                rw_half, ALU.mult,
+                y[h][:, ts, :].rearrange("p t (m e) -> p t m e", e=2),
+                floored[h][:, ts, :].rearrange("p t (m e) -> p t m e", e=2),
+                rw_half.to_broadcast([P, ts.stop - ts.start, JH // 2, 2]), ALU.mult,
             )
-            nc.sync.dma_start(dealt(out_0)[:, :, js], y[:])
-            tile = keep.tile([P, JH * PACK], BF16, name="y_bf%d" % h, align_bytes=64)
-            nc.scalar.copy(woven(tile), by_runs(y[:]))
-            y_bf.append(tile)
-        for h, js in halves():
-            nc.vector.quantize_mx(out=y_codes[:, js].bitcast(E4M3), scales=y_scales[:, js], in_=y_bf[h][:])
-            nc.sync.dma_start(out_words[:, js], y_codes[:, js].bitcast(I32))
+
+        def hand_out(h, cast):
+            nc.sync.dma_start(dealt(out_0)[:, :, cols[h]], y[h][:])
+            cast(woven(y_bf[h]), by_runs(y[h][:]))
+
+        def planes_out(h):
+            nc.vector.quantize_mx(out=y_codes[:, cols[h]].bitcast(E4M3), scales=y_scales[:, cols[h]], in_=y_bf[h][:])
+            nc.sync.dma_start(out_words[:, cols[h]], y_codes[:, cols[h]].bitcast(I32))
+
+        whole = slice(0, PACK)
+        floor_at(0, early)
+        weigh(0, early)
+        floor_at(0, late)
+        floor_at(1, whole)
+        weigh(0, late)
+        hand_out(0, nc.scalar.copy)
+        weigh(1, whole)
+        planes_out(0)
+        hand_out(1, nc.vector.tensor_copy)
+        planes_out(1)
         for q in range(4):
             queue = nc.sync if q < 2 else nc.scalar
             queue.dma_start(out_2[0, 4 * q : 4 * q + 4, :].bitcast(I32), y_scales[32 * q : 32 * q + 4, :].bitcast(I32))

@@ -103,7 +103,7 @@ def tile_list_sum_offsetpicks_largest_overtable_floored_pl_kernel(
         )
         w_sc_words = w_sc[:].rearrange("p n c -> p (n c)").bitcast(I32)
         for q in range(1, 4):
-            nc.sync.dma_start(w_sc_words[32 * q : 32 * q + 4, :], w_sc_words[4 * q : 4 * q + 4, :])
+            nc.gpsimd.dma_start(w_sc_words[32 * q : 32 * q + 4, :], w_sc_words[4 * q : 4 * q + 4, :])
 
         w_raw = load_words(w_words, "w_raw")
         w2_raw = load_words(w2_words, "w2_raw")

from contextlib import ExitStack

import concourse.mybir as mybir
from concourse.masks import make_identity

F32 = mybir.dt.float32
BF16 = mybir.dt.bfloat16
I32 = mybir.dt.int32
U32 = mybir.dt.uint32
U16 = mybir.dt.uint16
U8 = mybir.dt.uint8
E4M3 = mybir.dt.float8_e4m3fn_x4
E5M2 = mybir.dt.float8_e5m2_x4
ALU = mybir.AluOpType
ACT = mybir.ActivationFunctionType

P = 128
PACK = 4
J = 256
HALVES = 2
JH = J // HALVES
RUN = 4
COLS = 512

FLOPS = 3 * 2 * 512 * 512 * J


def tile_list_sum_offsetpicks_largest_overtable_floored_pl_kernel(
    tc, xf, ow, fk, w_words, w_scales, xo, fl, so, w2_words, w2_scales, tb, wb_words, wb_scales, tz, rw,
    offs, offs2, offs3, offs4, out_0, out_1, out_2,
):
    nc = tc.nc

    def dealt(dram):
        return dram.rearrange("(p t) c -> p t c", t=PACK)

    def by_runs(planes):
        return planes.rearrange("p t (c i) -> p c t i", i=RUN)

    def woven(tile):
        return tile[:].rearrange("p (c i t) -> p c t i", i=RUN, t=PACK)

    with ExitStack() as ctx:
        keep = ctx.enter_context(tc.tile_pool(name="keep", bufs=1))
        psum = ctx.enter_context(tc.psum_pool(name="psum", bufs=1))

        def load_list(dram, name):
            tile = keep.tile([P, J // 16], U16, name=name)
            nc.sync.dma_start(tile[:], dram)
            return tile

        def load_planes(dram, first, count, name):
            tile = keep.tile([P, count, dram.shape[1]], F32, name="%s%d" % (name, first))
            nc.sync.dma_start(tile[:], dealt(dram)[:, first : first + count, :])
            return tile

        def planes_of(tile):
            return [tile[:, t, :] for t in range(tile.shape[1])]

        def load_words(dram, name):
            tile = keep.tile([P, COLS], I32, name=name)
            nc.sync.dma_start(tile[:], dram[0].rearrange("p n t -> p (n t)").bitcast(I32))
            return tile

        def load_factor(dram, name):
            tile = keep.tile([P, PACK], F32, name=name)
            nc.gpsimd.dma_start(tile[:], dram.rearrange("(p t) o -> p (t o)", t=PACK))
            return tile

        def deal_words(raw, name):
            tile = keep.tile([P, PACK, P], U32, name=name, align_bytes=64)
            nc.scalar.copy(by_runs(tile[:]), raw[:].bitcast(U32).rearrange("p (c i t) -> p c t i", i=RUN, t=PACK))
            return tile

        def quantise(src, width, fmt, name):
            codes = keep.tile([P, width], U32, name=name + "_codes", align_bytes=64)
            scales = keep.tile([P, width], U8, name=name + "_scales", align_bytes=64)
            nc.vector.quantize_mx(out=codes[:].bitcast(fmt), scales=scales[:], in_=src[:])
            return codes, scales

        def halves():
            return [(h, slice(h * JH, (h + 1) * JH)) for h in range(HALVES)]

        scale_rows = keep.tile([P, 3, COLS], U8, name="scale_rows")
        nc.gpsimd.memset(scale_rows[:].bitcast(U32), 0)
        fk_sb = load_factor(fk, "fk_sb")
        fl_sb = load_factor(fl, "fl_sb")
        xf_sb = planes_of(load_planes(xf, 0, 2, "xf"))
        list1 = load_list(offs, "list1")
        for n, dram in enumerate((w_scales, w2_scales, wb_scales)):
            nc.sync.dma_start(scale_rows[0:16, n, :].bitcast(I32), dram[0].bitcast(I32))
        xf_sb = xf_sb + planes_of(load_planes(xf, 2, 2, "xf"))
        xo_sb = planes_of(load_planes(xo, 0, 1, "xo"))
        ow_sb = load_planes(ow, 0, PACK, "ow")
        list2 = load_list(offs2, "list2")
        xo_sb = xo_sb + planes_of(load_planes(xo, 1, 1, "xo"))
        so_sb = load_planes(so, 0, PACK, "so")
        xo_sb = xo_sb + planes_of(load_planes(xo, 2, 1, "xo")) + planes_of(load_planes(xo, 3, 1, "xo"))
        w_sc = keep.tile([P, 3, COLS], U8, name="w_sc", align_bytes=64)
        nc.vector.tensor_copy(
            w_sc[:].rearrange("p n (t m) -> p n t m", t=PACK),
            scale_rows[:].rearrange("p n (m t) -> p n t m", t=PACK),
        )
        w_sc_words = w_sc[:].rearrange("p n c -> p (n c)").bitcast(I32)
        for q in range(1, 4):
            nc.gpsimd.dma_start(w_sc_words[32 * q : 32 * q + 4, :], w_sc_words[4 * q : 4 * q + 4, :])

        w_raw = load_words(w_words, "w_raw")
        w2_raw = load_words(w2_words, "w2_raw")
        list3 = load_list(offs3, "list3")
        tb_sb = [planes_of(load_planes(tb, t, 1, "tb"))[0] for t in range(PACK)]
        wb_raw = load_words(wb_words, "wb_raw")
        list4 = load_list(offs4, "list4")
        tz_sb = [planes_of(load_planes(tz, t, 1, "tz"))[0] for t in range(PACK)]

        def pick(windows, offsets, name, split_last, on_vector=()):
            picked = keep.tile([P, PACK, J], F32, name=name)
            for t in range(PACK):
                if split_last and t == PACK - 1:
                    for h, js in halves():
                        nc.scalar.activation(picked[:, t, js], windows[t].indirect(offsets[:, h * JH // 16 : (h + 1) * JH // 16]), ACT.Copy)
                elif t in on_vector:
                    nc.vector.tensor_copy(picked[:, t, :], windows[t].indirect(offsets[:]))
                else:
                    nc.scalar.activation(picked[:, t, :], windows[t].indirect(offsets[:]), ACT.Copy)
            return picked

        rw_col = keep.tile([P, 2], F32, name="rw_col")
        nc.gpsimd.dma_start(rw_col[:], rw[0].rearrange("(p e) -> p e", e=2))
        ident = keep.tile([P, P], F32, name="ident")
        make_identity(nc, ident[:])
        rw_ps = psum.tile([P, 2, P], F32, name="rw_ps")
        for e in range(2):
            nc.tensor.transpose(rw_ps[:, e, :], rw_col[:, e : e + 1].to_broadcast([P, P]), ident[:])

        def factor(tile, width):
            return tile[:].unsqueeze(1).unsqueeze(3).to_broadcast([P, width // RUN, PACK, RUN])

        xf_pick = pick(xf_sb, list1, "xf_pick", False)
        diff = keep.tile([P, PACK, J], F32, name="diff")
        nc.vector.tensor_tensor(diff[:], xf_pick[:], ow_sb[:], ALU.subtract)
        u_bf = keep.tile([P, J * PACK], BF16, name="u_bf", align_bytes=64)
        nc.vector.tensor_tensor(woven(u_bf), by_runs(diff[:]), factor(fk_sb, J), ALU.mult)
        u_codes, u_scales = quantise(u_bf, J, E5M2, "u")

        xo_pick = pick(xo_sb, list2, "xo_pick", False)
        larger = keep.tile([P, PACK, J], F32, name="larger")
        for t in range(PACK):
            nc.vector.tensor_tensor(larger[:, t, :], xo_pick[:, t, :], so_sb[:, t, :], ALU.max)
        u2_bf = []
        for h, js in halves():
            tile = keep.tile([P, JH * PACK], BF16, name="u2_bf%d" % h, align_bytes=64)
            nc.vector.tensor_tensor(woven(tile), by_runs(larger[:, :, js]), factor(fl_sb, JH), ALU.mult)
            u2_bf.append(tile)
        u2_q = [quantise(u2_bf[h], JH, E4M3, "u2_%d" % h) for h, js in halves()]

        w_sb = deal_words(w_raw, "w_sb")
        w2_sb = deal_words(w2_raw, "w2_sb")

        def weight_scales(n, t):
            return w_sc[:, n, t * P : (t + 1) * P]

        a_ps = []
        for h, js in halves():
            bank = psum.tile([P, PACK, JH], F32, name="a_ps%d" % h)
            for t in range(PACK):
                nc.tensor.matmul_mx(
                    bank[:, t, :], lhsT=w_sb[:, t, :].bitcast(E5M2), lhsT_scale=weight_scales(0, t),
                    rhs=u_codes[:, js].bitcast(E5M2), rhs_scale=u_scales[:, js], start=(t == 0), stop=False,
                )
            a_ps.append(bank)
        for h, js in halves():
            codes, scales = u2_q[h]
            for t in range(PACK):
                nc.tensor.matmul_mx(
                    a_ps[h][:, t, :], lhsT=w2_sb[:, t, :].bitcast(E5M2), lhsT_scale=weight_scales(1, t),
                    rhs=codes[:].bitcast(E4M3), rhs_scale=scales[:], start=False, stop=(t == PACK - 1),
                )

        groups = (slice(0, PACK - 1), slice(PACK - 1, PACK))
        tb_pick = pick(tb_sb, list3, "tb_pick", True, on_vector=(2,))
        wb_sb = deal_words(wb_raw, "wb_sb")
        over = [keep.tile([P, PACK, JH], F32, name="over%d" % h) for h, js in halves()]
        hid_bf = [keep.tile([P, JH * PACK], BF16, name="hid_bf%d" % h, align_bytes=64) for h, js in halves()]
        p_ps = [psum.tile([P, PACK, JH], F32, name="p_ps%d" % h) for h, js in halves()]
        cols = [js for h, js in halves()]

        def take_off(h, ts):
            nc.vector.tensor_tensor(over[h][:, ts, :], a_ps[h][:, ts, :], tb_pick[:, ts, cols[h]], ALU.subtract)

        def keep_positive(h):
            nc.vector.tensor_scalar_max(woven(hid_bf[h]), by_runs(over[h][:]), 0.0)

        def second_layer(h):
            codes, scales = quantise(hid_bf[h], JH, E5M2, "hid%d" % h)
            for t in range(PACK):
                nc.tensor.matmul_mx(
                    p_ps[h][:, t, :], lhsT=wb_sb[:, t, :].bitcast(E4M3), lhsT_scale=weight_scales(2, t),
                    rhs=codes[:].bitcast(E5M2), rhs_scale=scales[:], start=True, stop=True,
                )

        early, late = groups
        take_off(0, early)
        take_off(0, late)
        take_off(1, early)
        keep_positive(0)
        take_off(1, late)
        second_layer(0)
        keep_positive(1)
        second_layer(1)

        tz_pick = pick(tz_sb, list4, "tz_pick", True)
        floored = [keep.tile([P, PACK, JH], F32, name="floored%d" % h) for h, js in halves()]
        y = [keep.tile([P, PACK, JH], F32, name="y%d" % h) for h, js in halves()]
        y_bf = [keep.tile([P, JH * PACK], BF16, name="y_bf%d" % h, align_bytes=64) for h, js in halves()]
        y_codes = keep.tile([P, J], U32, name="y_codes", align_bytes=64)
        y_scales = keep.tile([P, J], U8, name="y_scales", align_bytes=64)
        out_words = out_1[0].rearrange("p n t -> p (n t)").bitcast(I32)

        def floor_at(h, ts):
            nc.vector.tensor_tensor(floored[h][:, ts, :], p_ps[h][:, ts, :], tz_pick[:, ts, cols[h]], ALU.max)

        def weigh(h, ts):
            pairs = slice(h * JH // 2, (h + 1) * JH // 2)
            rw_half = rw_ps[:, :, pairs].rearrange("p e m -> p m e").unsqueeze(1)
            nc.vector.tensor_tensor(
                y[h][:, ts, :].rearrange("p t (m e) -> p t m e", e=2),
                floored[h][:, ts, :].rearrange("p t (m e) -> p t m e", e=2),
                rw_half.to_broadcast([P, ts.stop - ts.start, JH // 2, 2]), ALU.mult,
            )

        def hand_out(h, cast):
            nc.sync.dma_start(dealt(out_0)[:, :, cols[h]], y[h][:])
            cast(woven(y_bf[h]), by_runs(y[h][:]))

        def planes_out(h):
            nc.vector.quantize_mx(out=y_codes[:, cols[h]].bitcast(E4M3), scales=y_scales[:, cols[h]], in_=y_bf[h][:])
            nc.sync.dma_start(out_words[:, cols[h]], y_codes[:, cols[h]].bitcast(I32))

        whole = slice(0, PACK)
        floor_at(0, early)
        weigh(0, early)
        floor_at(0, late)
        floor_at(1, whole)
        weigh(0, late)
        hand_out(0, nc.scalar.copy)
        weigh(1, whole)
        planes_out(0)
        hand_out(1, nc.vector.tensor_copy)
        planes_out(1)
        for q in range(4):
            queue = nc.sync if q < 2 else nc.scalar
            queue.dma_start(out_2[0, 4 * q : 4 * q + 4, :].bitcast(I32), y_scales[32 * q : 32 * q + 4, :].bitcast(I32))
